import numpy as np
import ml_dtypes


def mxq(x, axis, fmt="e4m3"):
    dtype, down = {"e4m3": (ml_dtypes.float8_e4m3fn, 7), "e5m2": (ml_dtypes.float8_e5m2, 14)}[fmt]
    v = np.moveaxis(np.asarray(x, np.float32).astype(ml_dtypes.bfloat16).astype(np.float64), axis, -1)
    blocks = v.reshape(v.shape[:-1] + (-1, 32))
    amax = np.abs(blocks).max(-1, keepdims=True)
    byte = np.maximum(np.where(amax > 0, np.frexp(amax)[1] - 1 + 127, 0) - down, 1)
    scale = np.exp2(byte - 127.0)
    codes = (blocks / scale).astype(np.float32).astype(dtype).astype(np.float64)
    return np.moveaxis((codes * scale).reshape(v.shape), -1, axis)


WIDE = False


def mx_kscale(k):
    if not WIDE:
        return np.ones(k)
    levels = np.array([10, -10, 5, -5, 0])
    if k % 512:
        return np.exp2(np.random.permutation(np.resize(levels, k // 32))).repeat(32)
    a = np.empty((k // 512, 16))
    for p in range(k // 512):
        a[p, :8] = np.random.permutation(np.resize(levels, 8))
        for g in range(8):
            far = levels[np.abs(levels - a[p, g]) >= 10]
            a[p, g + 8] = far[np.random.randint(len(far))]
    return np.exp2(a.ravel()).repeat(32)


BF16 = ml_dtypes.bfloat16


def bf(x):
    return np.asarray(x, np.float32).astype(BF16)


def f64(x):
    return np.asarray(x).astype(np.float64)


E2M1 = np.array([0.0, 0.5, 1.0, 1.5, 2.0, 3.0, 4.0, 6.0, -0.0, -0.5, -1.0, -1.5, -2.0, -3.0, -4.0, -6.0])


def pack_weight(w, fmt):
    k, n = w.shape
    w = f64(bf(w)).reshape(k // 32, 32, n)
    amax = np.abs(w).max(1)
    if fmt == "e4m3":
        byte = np.frexp(amax)[1] - 1 + 127 - 7
    else:
        mant, ex = np.frexp(amax / 6.0)
        byte = np.where(mant > 0.5, ex, ex - 1) + 127
    byte = np.clip(np.where(amax > 0, byte, 1), 1, 254)
    scaled = (w * np.exp2(127.0 - byte)[:, None, :]).reshape(k, n).astype(np.float32)
    by_word = np.ascontiguousarray(scaled.reshape(k // 512, 128, 4, n).transpose(0, 1, 3, 2))
    if fmt == "e4m3":
        words = by_word.astype(ml_dtypes.float8_e4m3fn).view(np.uint8)
    else:
        c = by_word.astype(ml_dtypes.float4_e2m1fn).view(np.uint8) & 0xF
        words = c[..., 0::2] | (c[..., 1::2] << 4)
    return np.ascontiguousarray(words), np.ascontiguousarray(byte.astype(np.uint8).reshape(k // 512, 16, n))


def unpack_weight(words, scales, fmt):
    g, p, n, _ = words.shape
    if fmt == "e4m3":
        vals = np.ascontiguousarray(words).view(ml_dtypes.float8_e4m3fn).astype(np.float64)
    else:
        nib = np.empty((g, p, n, 4), np.uint8)
        nib[..., 0::2] = words & 0xF
        nib[..., 1::2] = words >> 4
        vals = E2M1[nib]
    vals = vals * np.repeat(np.exp2(scales.astype(np.float64) - 127.0), 8, axis=1)[..., None]
    return vals.transpose(0, 1, 3, 2).reshape(g * 512, n)
def pack4(w):
    words, scales = pack_weight(w, "e2m1")
    return words.reshape(words.shape[0], 128, -1), scales


def unpack4(words, scales):
    return unpack_weight(words.reshape(words.shape[0], 128, -1, 2), scales, "e2m1")


def planes(Y):
    n, m = Y.shape
    b = f64(bf(Y)).reshape(n // 32, 32, m)
    amax = np.abs(b).max(1)
    byte = np.clip(np.where(amax > 0, np.frexp(amax)[1] - 1 + 127 - 7, 1), 1, 254)
    codes = (b * np.exp2(127.0 - byte)[:, None, :]).reshape(n, m).astype(np.float32).astype(ml_dtypes.float8_e4m3fn).view(np.uint8)
    words = codes.reshape(n // 512, 128, 4, m).transpose(0, 1, 3, 2)
    return np.ascontiguousarray(words), np.ascontiguousarray(byte.astype(np.uint8).reshape(n // 512, 16, m))


T, D, F = 512, 1024, 3072
CORR = 0.33


def setup_inputs():
    s, t1, t0 = mx_kscale(D), mx_kscale(D), mx_kscale(D)
    upstream = bf(np.random.randn(T, D) * s)
    block2 = bf(CORR * np.random.randn(D, D) / np.sqrt(D) * t1[:, None] / s[None, :])
    gain2 = bf((1 + 0.1 * np.random.randn(D)) * t1 / s)
    block1 = bf(CORR * np.random.randn(D, D) / np.sqrt(D) * t0[:, None] / t1[None, :])
    gain1 = bf((1 + 0.1 * np.random.randn(D)) * t0 / t1)
    dec = np.random.randn(F, D) / np.sqrt(D)
    dec_words, dec_scales = pack4(dec.T / t0[:, None])
    z = bf((1.2 + 0.8 * np.random.randn(T, F)) * np.exp(0.8 * np.random.randn(F)))
    return {"upstream": upstream, "block2": block2, "gain2": gain2, "block1": block1, "gain1": gain1,
            "dec_words": dec_words, "dec_scales": dec_scales, "z": z}

def reference(upstream, block2, gain2, block1, gain1, dec_words, dec_scales, z):
    U, B2, a2, B1, a1, Z = f64(upstream), f64(block2), f64(gain2), f64(block1), f64(gain1), f64(z)
    C = unpack4(dec_words, dec_scales)
    H1 = U * a2 + (mxq(U, 1, "e4m3") @ mxq(B2, 1, "e4m3").T)
    H0 = H1 * a1 + (mxq(H1, 1, "e4m3") @ mxq(B1, 1, "e4m3").T)
    y = np.maximum(Z, 0.0) * (mxq(H0, 1, "e4m3") @ C)
    Y = y.T
    words, scales = planes(Y)
    return y, words, scales

@@ -1,0 +1,437 @@
+from contextlib import ExitStack
+
+import concourse.mybir as mybir
+from concourse.masks import make_identity
+
+T, D, F = 512, 1024, 3072
+FLOPS = 2 * T * D * (2 * D + F)
+
+F32 = mybir.dt.float32
+BF16 = mybir.dt.bfloat16
+U32 = mybir.dt.uint32
+I32 = mybir.dt.int32
+U8 = mybir.dt.uint8
+FP8X4 = mybir.dt.float8_e4m3fn_x4
+FP4X4 = mybir.dt.float4_e2m1fn_x4
+ALU = mybir.AluOpType
+
+P = 128
+KP = 512
+GD = D // KP
+GF = F // KP
+HT = T // 2
+CW = 1024
+NC = F // CW
+
+
+def tile_sae_feature_attribution_k1_kernel(
+    tc, upstream, block2, gain2, block1, gain1, dec_words, dec_scales, z, out_0, out_1, out_2
+):
+    nc = tc.nc
+    with ExitStack() as ctx:
+        keep = ctx.enter_context(tc.tile_pool(name="keep", bufs=1))
+        stage = ctx.enter_context(tc.tile_pool(name="stage", bufs=3))
+        psum = ctx.enter_context(tc.psum_pool(name="psum", bufs=8))
+        ctx.enter_context(tc.manual_schedule())
+
+        def kept(name, shape, dtype):
+            return keep.tile(shape, dtype, name=name, align_bytes=64)
+
+        def new_bank():
+            return psum.tile([P, KP], F32, name="bank", tag="bank")
+
+        ident = kept("ident", [P, P], F32)
+        gains = [kept("gain%d" % s, [P, GD, 4], BF16) for s in range(2)]
+        u_raw = [kept("u_raw%d" % j, [P, D], BF16) for j in range(4)]
+        b_raw = [[kept("b_raw%d_%d" % (s, q), [P, 2, D], BF16) for q in range(4)] for s in range(2)]
+        b_codes = [[kept("b_codes%d_%d" % (s, q), [P, 2, GD, P], U32) for q in range(4)] for s in range(2)]
+        b_scales = [[kept("b_scales%d_%d" % (s, q), [P, 2, GD, P], U8) for q in range(4)] for s in range(2)]
+        c_words = [kept("c_words%d" % c, [P, GD, 2 * CW], U8) for c in range(NC)]
+        c_scales = kept("c_scales", [P, GD, F], U8)
+        z_sb = [[kept("z%d_%d" % (h, c), [P, 2, CW], BF16) for c in range(NC)] for h in range(2)]
+        act = [[kept("act%d_%d" % (s, h), [P, GD, HT, 4], BF16) for h in range(2)] for s in range(3)]
+        act_codes = [[kept("act_codes%d_%d" % (s, h), [P, GD, HT], U32) for h in range(2)] for s in range(3)]
+        act_scales = [[kept("act_scales%d_%d" % (s, h), [P, GD, HT], U8) for h in range(2)] for s in range(3)]
+        rows = [[kept("rows%d_%d" % (s, h), [P, GD, 4, HT], (F32, BF16)[s]) for h in range(2)] for s in range(2)]
+        y_scales = [kept("y_scales%d" % h, [P, GF, HT], U8) for h in range(2)]
+
+        nc.vector.memset(c_scales[:].rearrange("p g n -> p (g n)").bitcast(U32), 0)
+        make_identity(nc, ident[:])
+        for s, gain in enumerate((gain2, gain1)):
+            nc.scalar.dma_start(out=gains[s][:], in_=gain.rearrange("(g p t) -> p g t", g=GD, t=4))
+
+        def load_u(j):
+            nc.sync.dma_start(out=u_raw[j][:], in_=upstream[j * P : (j + 1) * P, :])
+
+        def load_b(s, q):
+            g, pair = divmod(q, 2)
+            src = (block2, block1)[s][g * KP : (g + 1) * KP, :].rearrange("(m t) k -> m t k", t=4)
+            nc.sync.dma_start(out=b_raw[s][q][:], in_=src[:, 2 * pair : 2 * pair + 2, :])
+
+        def load_c(c):
+            src = dec_words.rearrange("g p b -> p g b")[:, :, 2 * CW * c : 2 * CW * (c + 1)]
+            nc.sync.dma_start(out=c_words[c][:].bitcast(I32), in_=src.bitcast(I32))
+
+        def load_z(h, c):
+            src = z[h * HT : (h + 1) * HT, c * CW : (c + 1) * CW].rearrange("(i p) f -> p i f", i=2)
+            nc.sync.dma_start(out=z_sb[h][c][:], in_=src)
+
+        def load_c_scales():
+            for quad in range(4):
+                src = dec_scales[:, 4 * quad : 4 * quad + 4, :].rearrange("g r n -> r g n")
+                nc.sync.dma_start(out=c_scales[32 * quad : 32 * quad + 4, :, :].bitcast(I32), in_=src.bitcast(I32))
+
+        def turn(raw, dest):
+            words = raw.bitcast(F32)
+            bank = new_bank()
+            for g in range(GD):
+                for u in range(2):
+                    at = (2 * g + u) * P
+                    nc.tensor.transpose(bank[:, at : at + P], words[:, 2 * P * g + u : 2 * P * (g + 1) : 2], ident[:])
+            nc.scalar.copy(out=dest.bitcast(F32), in_=bank[:].rearrange("p (g u r) -> p g r u", g=GD, u=2))
+
+        def quantize(codes, scales, src):
+            nc.vector.quantize_mx(out=codes.bitcast(FP8X4), scales=scales, in_=src)
+
+        def turn_u(h):
+            for i in range(2):
+                turn(u_raw[2 * h + i][:], act[0][h][:, :, i * P : (i + 1) * P, :])
+
+        b_turned = {}
+
+        def turn_b(s, q):
+            b_turned[s, q] = stage.tile([P, 2, GD, P, 4], BF16, name="b_turned", bufs=4, align_bytes=64)
+            for i in range(2):
+                turn(b_raw[s][q][:, i, :], b_turned[s, q][:, i, :, :, :])
+
+        def quantize_b(s, q):
+            quantize(
+                b_codes[s][q][:].rearrange("p i g r -> p (i g r)"),
+                b_scales[s][q][:].rearrange("p i g r -> p (i g r)"),
+                b_turned[s, q][:].rearrange("p i g r t -> p (i g r t)"),
+            )
+
+        def quantize_act(s, h, g):
+            quantize(act_codes[s][h][:, g, :], act_scales[s][h][:, g, :], act[s][h][:, g, :, :].rearrange("p n t -> p (n t)"))
+
+        banks = {}
+
+        def block_matmul(s, h, q):
+            banks[s, h, q] = new_bank()
+            for i in range(2):
+                for g in range(GD):
+                    nc.tensor.matmul_mx(
+                        out=banks[s, h, q][:, i * HT : (i + 1) * HT],
+                        lhsT=b_codes[s][q][:, i, g, :].bitcast(FP8X4),
+                        lhsT_scale=b_scales[s][q][:, i, g, :],
+                        rhs=act_codes[s][h][:, g, :].bitcast(FP8X4),
+                        rhs_scale=act_scales[s][h][:, g, :],
+                        start=(g == 0),
+                        stop=(g == GD - 1),
+                    )
+
+        def block_residual(s, h, q):
+            g, pair = divmod(q, 2)
+            for i in range(2):
+                t = 2 * pair + i
+                src = act[0][h][:, g, :, t] if s == 0 else rows[0][h][:, g, t, :]
+                nc.vector.scalar_tensor_tensor(
+                    out=rows[s][h][:, g, t, :],
+                    in0=src,
+                    scalar=gains[s][:, g, t : t + 1],
+                    in1=banks[s, h, q][:, i * HT : (i + 1) * HT],
+                    op0=ALU.mult,
+                    op1=ALU.add,
+                )
+
+        def interleave(copy, s, h, g):
+            copy(out=act[s + 1][h][:, g, :, :], in_=rows[s][h][:, g, :, :].rearrange("p t n -> p n t"))
+
+        y_sb, y_bf, y_turned, y_bank, y_codes = {}, {}, {}, {}, {}
+
+        def feature_matmul(h, g, i):
+            c, at = divmod(g * KP, CW)
+            y_bank[h, g, i] = new_bank()
+            for k in range(GD):
+                nc.tensor.matmul_mx(
+                    out=y_bank[h, g, i][:],
+                    lhsT=act_codes[2][h][:, k, i * P : (i + 1) * P].bitcast(FP8X4),
+                    lhsT_scale=act_scales[2][h][:, k, i * P : (i + 1) * P],
+                    rhs=c_words[c][:, k, 2 * at : 2 * (at + KP)].bitcast(FP4X4),
+                    rhs_scale=c_scales[:, k, g * KP : (g + 1) * KP],
+                    start=(k == 0),
+                    stop=(k == GD - 1),
+                )
+
+        def attribute(h, g, i):
+            c, at = divmod(g * KP, CW)
+            if i == 0:
+                y_sb[h, g] = stage.tile([P, 2, KP], F32, name="y_sb", bufs=6, align_bytes=64)
+            nc.vector.scalar_tensor_tensor(
+                out=y_sb[h, g][:, i, :],
+                in0=z_sb[h][c][:, i, at : at + KP],
+                scalar=0.0,
+                in1=y_bank[h, g, i][:],
+                op0=ALU.max,
+                op1=ALU.mult,
+            )
+
+        def store_y(h, g):
+            dst = out_0[h * HT : (h + 1) * HT, g * KP : (g + 1) * KP].rearrange("(i p) f -> p i f", i=2)
+            nc.sync.dma_start(out=dst, in_=y_sb[h, g][:])
+
+        def round_y(copy, h, g, i):
+            if i == 0:
+                y_bf[h, g] = stage.tile([P, 2, 2, P, 2], BF16, name="y_bf", bufs=5, align_bytes=64)
+            copy(out=y_bf[h, g][:, i, :, :, :], in_=y_sb[h, g][:, i, :].rearrange("p (m u e) -> p u m e", u=2, e=2))
+
+        def turn_y(h, g):
+            words = y_bf[h, g][:].rearrange("p i u m e -> p (i u m e)").bitcast(F32)
+            y_bank[h, g] = new_bank()
+            for w in range(4):
+                nc.tensor.transpose(y_bank[h, g][:, w * P : (w + 1) * P], words[:, w * P : (w + 1) * P], ident[:])
+
+        def drain_y(h, g):
+            y_turned[h, g] = stage.tile([P, 2, P, 4], BF16, name="y_turned", bufs=4, align_bytes=64)
+            nc.scalar.copy(out=y_turned[h, g][:].bitcast(F32), in_=y_bank[h, g][:].rearrange("p (i u r) -> p i r u", i=2, u=2))
+
+        def quantize_y(h, g):
+            y_codes[h, g] = stage.tile([P, HT], U32, name="y_codes", bufs=4, align_bytes=64)
+            quantize(y_codes[h, g][:], y_scales[h][:, g, :], y_turned[h, g][:].rearrange("p i r t -> p (i r t)"))
+
+        def store_y_words(h, g):
+            dst = out_1[g].rearrange("p m t -> p (m t)")[:, 4 * HT * h : 4 * HT * (h + 1)]
+            nc.sync.dma_start(out=dst.bitcast(I32), in_=y_codes[h, g][:].bitcast(I32))
+
+        def store_y_scales(h):
+            for quad in range(4):
+                dst = out_2[:, 4 * quad : 4 * quad + 4, h * HT : (h + 1) * HT].rearrange("g r m -> r g m")
+                nc.sync.dma_start(out=dst.bitcast(I32), in_=y_scales[h][32 * quad : 32 * quad + 4, :, :].bitcast(I32))
+
+        on_scalar, on_vector = nc.scalar.copy, nc.vector.tensor_copy
+        load_u(0)
+        load_u(1)
+        load_b(0, 0)
+        load_b(0, 1)
+        load_b(0, 2)
+        load_u(2)
+        load_u(3)
+        load_b(0, 3)
+        load_b(1, 0)
+        load_b(1, 1)
+        load_b(1, 2)
+        load_b(1, 3)
+        load_c_scales()
+        load_c(0)
+        load_z(0, 0)
+        load_c(1)
+        load_z(0, 1)
+        load_c(2)
+        load_z(0, 2)
+        load_z(1, 0)
+        load_z(1, 1)
+        load_z(1, 2)
+        turn_u(0)
+        quantize_act(0, 0, 0)
+        quantize_act(0, 0, 1)
+        turn_b(0, 0)
+        quantize_b(0, 0)
+        turn_b(0, 1)
+        quantize_b(0, 1)
+        turn_b(0, 2)
+        quantize_b(0, 2)
+        turn_u(1)
+        block_matmul(0, 0, 0)
+        block_residual(0, 0, 0)
+        quantize_act(0, 1, 0)
+        quantize_act(0, 1, 1)
+        turn_b(0, 3)
+        quantize_b(0, 3)
+        turn_b(1, 0)
+        block_matmul(0, 0, 1)
+        block_residual(0, 0, 1)
+        block_matmul(0, 0, 2)
+        block_residual(0, 0, 2)
+        interleave(on_scalar, 0, 0, 0)
+        block_matmul(0, 0, 3)
+        block_residual(0, 0, 3)
+        block_matmul(0, 1, 0)
+        block_residual(0, 1, 0)
+        quantize_b(1, 0)
+        quantize_act(1, 0, 0)
+        interleave(on_scalar, 0, 0, 1)
+        block_matmul(0, 1, 1)
+        block_residual(0, 1, 1)
+        block_matmul(0, 1, 2)
+        block_residual(0, 1, 2)
+        block_matmul(0, 1, 3)
+        block_residual(0, 1, 3)
+        turn_b(1, 1)
+        quantize_act(1, 0, 1)
+        interleave(on_vector, 0, 1, 0)
+        turn_b(1, 2)
+        quantize_b(1, 1)
+        quantize_act(1, 1, 0)
+        turn_b(1, 3)
+        quantize_b(1, 2)
+        interleave(on_scalar, 0, 1, 1)
+        block_matmul(1, 0, 0)
+        block_residual(1, 0, 0)
+        quantize_b(1, 3)
+        block_matmul(1, 0, 1)
+        block_residual(1, 0, 1)
+        quantize_act(1, 1, 1)
+        interleave(on_scalar, 1, 0, 0)
+        block_matmul(1, 0, 2)
+        block_residual(1, 0, 2)
+        block_matmul(1, 0, 3)
+        block_residual(1, 0, 3)
+        block_matmul(1, 1, 0)
+        block_residual(1, 1, 0)
+        block_matmul(1, 1, 1)
+        block_matmul(1, 1, 2)
+        block_matmul(1, 1, 3)
+        interleave(on_vector, 1, 0, 1)
+        quantize_act(2, 0, 0)
+        quantize_act(2, 0, 1)
+        block_residual(1, 1, 1)
+        block_residual(1, 1, 2)
+        interleave(on_scalar, 1, 1, 0)
+        feature_matmul(0, 0, 0)
+        feature_matmul(0, 0, 1)
+        attribute(0, 0, 0)
+        attribute(0, 0, 1)
+        store_y(0, 0)
+        round_y(on_scalar, 0, 0, 0)
+        round_y(on_scalar, 0, 0, 1)
+        block_residual(1, 1, 3)
+        feature_matmul(0, 1, 0)
+        feature_matmul(0, 1, 1)
+        attribute(0, 1, 0)
+        attribute(0, 1, 1)
+        store_y(0, 1)
+        round_y(on_scalar, 0, 1, 0)
+        interleave(on_scalar, 1, 1, 1)
+        feature_matmul(0, 2, 0)
+        feature_matmul(0, 2, 1)
+        attribute(0, 2, 0)
+        round_y(on_vector, 0, 1, 1)
+        quantize_act(2, 1, 0)
+        attribute(0, 2, 1)
+        store_y(0, 2)
+        round_y(on_scalar, 0, 2, 0)
+        round_y(on_scalar, 0, 2, 1)
+        feature_matmul(0, 3, 0)
+        feature_matmul(0, 3, 1)
+        turn_y(0, 0)
+        turn_y(0, 1)
+        attribute(0, 3, 0)
+        attribute(0, 3, 1)
+        store_y(0, 3)
+        round_y(on_scalar, 0, 3, 0)
+        drain_y(0, 0)
+        feature_matmul(0, 4, 0)
+        feature_matmul(0, 4, 1)
+        attribute(0, 4, 0)
+        round_y(on_vector, 0, 3, 1)
+        quantize_act(2, 1, 1)
+        attribute(0, 4, 1)
+        store_y(0, 4)
+        round_y(on_scalar, 0, 4, 0)
+        drain_y(0, 1)
+        round_y(on_scalar, 0, 4, 1)
+        feature_matmul(0, 5, 0)
+        feature_matmul(0, 5, 1)
+        turn_y(0, 2)
+        turn_y(0, 3)
+        attribute(0, 5, 0)
+        quantize_y(0, 0)
+        store_y_words(0, 0)
+        attribute(0, 5, 1)
+        store_y(0, 5)
+        round_y(on_scalar, 0, 5, 0)
+        drain_y(0, 2)
+        feature_matmul(1, 0, 0)
+        feature_matmul(1, 0, 1)
+        attribute(1, 0, 0)
+        round_y(on_vector, 0, 5, 1)
+        quantize_y(0, 1)
+        store_y_words(0, 1)
+        attribute(1, 0, 1)
+        store_y(1, 0)
+        round_y(on_scalar, 1, 0, 0)
+        drain_y(0, 3)
+        round_y(on_scalar, 1, 0, 1)
+        feature_matmul(1, 1, 0)
+        feature_matmul(1, 1, 1)
+        turn_y(0, 4)
+        turn_y(0, 5)
+        attribute(1, 1, 0)
+        quantize_y(0, 2)
+        store_y_words(0, 2)
+        attribute(1, 1, 1)
+        store_y(1, 1)
+        round_y(on_scalar, 1, 1, 0)
+        drain_y(0, 4)
+        feature_matmul(1, 2, 0)
+        feature_matmul(1, 2, 1)
+        attribute(1, 2, 0)
+        round_y(on_vector, 1, 1, 1)
+        quantize_y(0, 3)
+        store_y_words(0, 3)
+        attribute(1, 2, 1)
+        store_y(1, 2)
+        round_y(on_scalar, 1, 2, 0)
+        drain_y(0, 5)
+        round_y(on_scalar, 1, 2, 1)
+        feature_matmul(1, 3, 0)
+        feature_matmul(1, 3, 1)
+        turn_y(1, 0)
+        turn_y(1, 1)
+        attribute(1, 3, 0)
+        quantize_y(0, 4)
+        store_y_words(0, 4)
+        attribute(1, 3, 1)
+        store_y(1, 3)
+        round_y(on_scalar, 1, 3, 0)
+        drain_y(1, 0)
+        feature_matmul(1, 4, 0)
+        feature_matmul(1, 4, 1)
+        attribute(1, 4, 0)
+        round_y(on_vector, 1, 3, 1)
+        quantize_y(0, 5)
+        store_y_words(0, 5)
+        store_y_scales(0)
+        attribute(1, 4, 1)
+        store_y(1, 4)
+        round_y(on_scalar, 1, 4, 0)
+        drain_y(1, 1)
+        feature_matmul(1, 5, 0)
+        feature_matmul(1, 5, 1)
+        turn_y(1, 2)
+        turn_y(1, 3)
+        attribute(1, 5, 0)
+        round_y(on_vector, 1, 4, 1)
+        quantize_y(1, 0)
+        store_y_words(1, 0)
+        attribute(1, 5, 1)
+        store_y(1, 5)
+        round_y(on_scalar, 1, 5, 0)
+        drain_y(1, 2)
+        round_y(on_vector, 1, 5, 1)
+        turn_y(1, 4)
+        turn_y(1, 5)
+        quantize_y(1, 1)
+        store_y_words(1, 1)
+        drain_y(1, 3)
+        quantize_y(1, 2)
+        store_y_words(1, 2)
+        drain_y(1, 4)
+        quantize_y(1, 3)
+        store_y_words(1, 3)
+        drain_y(1, 5)
+        quantize_y(1, 4)
+        store_y_words(1, 4)
+        quantize_y(1, 5)
+        store_y_words(1, 5)
+        store_y_scales(1)

@@ -46,9 +46,10 @@ def tile_sae_feature_attribution_k1_kernel(
         b_raw = [[kept("b_raw%d_%d" % (s, q), [P, 2, D], BF16) for q in range(4)] for s in range(2)]
         b_codes = [[kept("b_codes%d_%d" % (s, q), [P, 2, GD, P], U32) for q in range(4)] for s in range(2)]
         b_scales = [[kept("b_scales%d_%d" % (s, q), [P, 2, GD, P], U8) for q in range(4)] for s in range(2)]
-        c_words = [kept("c_words%d" % c, [P, GD, 2 * CW], U8) for c in range(NC)]
+        c_words = [kept("c_words%d" % c, [P, GD, 2 * width], U8) for c, width in enumerate((CW, F - CW))]
         c_scales = kept("c_scales", [P, GD, F], U8)
-        z_sb = [[kept("z%d_%d" % (h, c), [P, 2, CW], BF16) for c in range(NC)] for h in range(2)]
+        z_first = [kept("z_first%d" % c, [P, 2, width], BF16) for c, width in enumerate((CW, F - CW))]
+        z_second = [kept("z_second%d" % i, [P, F], BF16) for i in range(2)]
         act = [[kept("act%d_%d" % (s, h), [P, GD, HT, 4], BF16) for h in range(2)] for s in range(3)]
         act_codes = [[kept("act_codes%d_%d" % (s, h), [P, GD, HT], U32) for h in range(2)] for s in range(3)]
         act_scales = [[kept("act_scales%d_%d" % (s, h), [P, GD, HT], U8) for h in range(2)] for s in range(3)]
@@ -69,12 +70,16 @@ def tile_sae_feature_attribution_k1_kernel(
             nc.sync.dma_start(out=b_raw[s][q][:], in_=src[:, 2 * pair : 2 * pair + 2, :])
 
         def load_c(c):
-            src = dec_words.rearrange("g p b -> p g b")[:, :, 2 * CW * c : 2 * CW * (c + 1)]
+            cols = (slice(0, 2 * CW), slice(2 * CW, 2 * F))[c]
+            src = dec_words.rearrange("g p b -> p g b")[:, :, cols]
             nc.sync.dma_start(out=c_words[c][:].bitcast(I32), in_=src.bitcast(I32))
 
         def load_z(h, c):
-            src = z[h * HT : (h + 1) * HT, c * CW : (c + 1) * CW].rearrange("(i p) f -> p i f", i=2)
-            nc.sync.dma_start(out=z_sb[h][c][:], in_=src)
+            if h == 0:
+                cols = (slice(0, CW), slice(CW, F))[c]
+                nc.sync.dma_start(out=z_first[c][:], in_=z[:HT, cols].rearrange("(i p) f -> p i f", i=2))
+            else:
+                nc.sync.dma_start(out=z_second[c][:], in_=z[HT + c * P : HT + (c + 1) * P, :])
 
         def load_c_scales():
             for quad in range(4):
@@ -114,6 +119,13 @@ def tile_sae_feature_attribution_k1_kernel(
         def quantize_act(s, h, g):
             quantize(act_codes[s][h][:, g, :], act_scales[s][h][:, g, :], act[s][h][:, g, :, :].rearrange("p n t -> p (n t)"))
 
+        def quantize_u(h):
+            quantize(
+                act_codes[0][h][:].rearrange("p g n -> p (g n)"),
+                act_scales[0][h][:].rearrange("p g n -> p (g n)"),
+                act[0][h][:].rearrange("p g n t -> p (g n t)"),
+            )
+
         banks = {}
 
         def block_matmul(s, h, q):
@@ -149,66 +161,84 @@ def tile_sae_feature_attribution_k1_kernel(
 
         y_sb, y_bf, y_turned, y_bank, y_codes = {}, {}, {}, {}, {}
 
-        def feature_matmul(h, g, i):
-            c, at = divmod(g * KP, CW)
-            y_bank[h, g, i] = new_bank()
-            for k in range(GD):
+        def feature_matmul(h, k, i, j):
+            f0 = k * CW + j * KP
+            c = min(k, 1)
+            at = f0 - c * CW
+            y_bank[h, k, i, j] = new_bank()
+            for g in range(GD):
                 nc.tensor.matmul_mx(
-                    out=y_bank[h, g, i][:],
-                    lhsT=act_codes[2][h][:, k, i * P : (i + 1) * P].bitcast(FP8X4),
-                    lhsT_scale=act_scales[2][h][:, k, i * P : (i + 1) * P],
-                    rhs=c_words[c][:, k, 2 * at : 2 * (at + KP)].bitcast(FP4X4),
-                    rhs_scale=c_scales[:, k, g * KP : (g + 1) * KP],
-                    start=(k == 0),
-                    stop=(k == GD - 1),
+                    out=y_bank[h, k, i, j][:],
+                    lhsT=act_codes[2][h][:, g, i * P : (i + 1) * P].bitcast(FP8X4),
+                    lhsT_scale=act_scales[2][h][:, g, i * P : (i + 1) * P],
+                    rhs=c_words[c][:, g, 2 * at : 2 * (at + KP)].bitcast(FP4X4),
+                    rhs_scale=c_scales[:, g, f0 : f0 + KP],
+                    start=(g == 0),
+                    stop=(g == GD - 1),
                 )
 
-        def attribute(h, g, i):
-            c, at = divmod(g * KP, CW)
-            if i == 0:
-                y_sb[h, g] = stage.tile([P, 2, KP], F32, name="y_sb", bufs=6, align_bytes=64)
+        def attribute(h, k, i, j):
+            f0 = k * CW + j * KP
+            c = min(k, 1)
+            at = f0 - c * CW
+            if j == 0:
+                y_sb[h, k, i] = stage.tile([P, 2, KP], F32, name="y_sb", bufs=5, align_bytes=64)
             nc.vector.scalar_tensor_tensor(
-                out=y_sb[h, g][:, i, :],
-                in0=z_sb[h][c][:, i, at : at + KP],
+                out=y_sb[h, k, i][:, j, :],
+                in0=z_first[c][:, i, at : at + KP] if h == 0 else z_second[i][:, f0 : f0 + KP],
                 scalar=0.0,
-                in1=y_bank[h, g, i][:],
+                in1=y_bank[h, k, i, j][:],
                 op0=ALU.max,
                 op1=ALU.mult,
             )
 
-        def store_y(h, g):
-            dst = out_0[h * HT : (h + 1) * HT, g * KP : (g + 1) * KP].rearrange("(i p) f -> p i f", i=2)
-            nc.sync.dma_start(out=dst, in_=y_sb[h, g][:])
+        def store_y(h, k, i, j0, j1):
+            r0, f0 = h * HT + i * P, k * CW
+            src = y_sb[h, k, i][:, j0:j1, :].rearrange("p j f -> p (j f)")
+            nc.sync.dma_start(out=out_0[r0 : r0 + P, f0 + j0 * KP : f0 + j1 * KP], in_=src)
 
-        def round_y(copy, h, g, i):
+        def round_y(copy, h, k, i, j):
+            y_bf[h, k, i, j] = stage.tile([P, 2, P, 2], BF16, name="y_bf", bufs=8, align_bytes=64)
+            copy(out=y_bf[h, k, i, j][:], in_=y_sb[h, k, i][:, j, :].rearrange("p (m u e) -> p u m e", u=2, e=2))
+
+        def turn_y(h, k, i):
+            y_bank[h, k, i] = new_bank()
+            for j in range(2):
+                words = y_bf[h, k, i, j][:].rearrange("p u m e -> p (u m e)").bitcast(F32)
+                for u in range(2):
+                    at = (2 * j + u) * P
+                    nc.tensor.transpose(y_bank[h, k, i][:, at : at + P], words[:, u * P : (u + 1) * P], ident[:])
+
+        def drain_y(copy, h, k, i):
             if i == 0:
-                y_bf[h, g] = stage.tile([P, 2, 2, P, 2], BF16, name="y_bf", bufs=5, align_bytes=64)
-            copy(out=y_bf[h, g][:, i, :, :, :], in_=y_sb[h, g][:, i, :].rearrange("p (m u e) -> p u m e", u=2, e=2))
+                y_turned[h, k] = stage.tile([P, 2, 2, P, 4], BF16, name="y_turned", align_bytes=64)
+            src = y_bank[h, k, i][:].rearrange("p (j u r) -> p j r u", j=2, u=2)
+            copy(out=y_turned[h, k][:, :, i, :, :].bitcast(F32), in_=src)
 
-        def turn_y(h, g):
-            words = y_bf[h, g][:].rearrange("p i u m e -> p (i u m e)").bitcast(F32)
-            y_bank[h, g] = new_bank()
-            for w in range(4):
-                nc.tensor.transpose(y_bank[h, g][:, w * P : (w + 1) * P], words[:, w * P : (w + 1) * P], ident[:])
+        def quantize_y(h, k, j0, j1):
+            if j0 == 0:
+                y_codes[h, k] = stage.tile([P, 2, HT], U32, name="y_codes", align_bytes=64)
+            quantize(
+                y_codes[h, k][:, j0:j1, :].rearrange("p j m -> p (j m)"),
+                y_scales[h][:, 2 * k + j0 : 2 * k + j1, :].rearrange("p j m -> p (j m)"),
+                y_turned[h, k][:, j0:j1, :, :, :].rearrange("p j i r t -> p (j i r t)"),
+            )
 
-        def drain_y(h, g):
-            y_turned[h, g] = stage.tile([P, 2, P, 4], BF16, name="y_turned", bufs=4, align_bytes=64)
-            nc.scalar.copy(out=y_turned[h, g][:].bitcast(F32), in_=y_bank[h, g][:].rearrange("p (i u r) -> p i r u", i=2, u=2))
-
-        def quantize_y(h, g):
-            y_codes[h, g] = stage.tile([P, HT], U32, name="y_codes", bufs=4, align_bytes=64)
-            quantize(y_codes[h, g][:], y_scales[h][:, g, :], y_turned[h, g][:].rearrange("p i r t -> p (i r t)"))
-
-        def store_y_words(h, g):
-            dst = out_1[g].rearrange("p m t -> p (m t)")[:, 4 * HT * h : 4 * HT * (h + 1)]
-            nc.sync.dma_start(out=dst.bitcast(I32), in_=y_codes[h, g][:].bitcast(I32))
+        def store_y_words(h, k, j0, j1):
+            dst = out_1[2 * k + j0 : 2 * k + j1].rearrange("g p m t -> p g (m t)")[:, :, 4 * HT * h : 4 * HT * (h + 1)]
+            nc.sync.dma_start(out=dst.bitcast(I32), in_=y_codes[h, k][:, j0:j1, :].bitcast(I32))
 
         def store_y_scales(h):
             for quad in range(4):
                 dst = out_2[:, 4 * quad : 4 * quad + 4, h * HT : (h + 1) * HT].rearrange("g r m -> r g m")
-                nc.sync.dma_start(out=dst.bitcast(I32), in_=y_scales[h][32 * quad : 32 * quad + 4, :, :].bitcast(I32))
+                queue = nc.scalar if h == 1 and quad >= 2 else nc.sync
+                queue.dma_start(out=dst.bitcast(I32), in_=y_scales[h][32 * quad : 32 * quad + 4, :, :].bitcast(I32))
 
         on_scalar, on_vector = nc.scalar.copy, nc.vector.tensor_copy
+
+        def on_pool(out, in_):
+            nc.gpsimd.tensor_scalar(out=out, in0=in_, scalar1=1.0, scalar2=1.0, op0=ALU.mult, op1=ALU.mult)
+
         load_u(0)
         load_u(1)
         load_b(0, 0)
@@ -226,14 +256,10 @@ def tile_sae_feature_attribution_k1_kernel(
         load_z(0, 0)
         load_c(1)
         load_z(0, 1)
-        load_c(2)
-        load_z(0, 2)
         load_z(1, 0)
         load_z(1, 1)
-        load_z(1, 2)
         turn_u(0)
-        quantize_act(0, 0, 0)
-        quantize_act(0, 0, 1)
+        quantize_u(0)
         turn_b(0, 0)
         quantize_b(0, 0)
         turn_b(0, 1)
@@ -241,197 +267,187 @@ def tile_sae_feature_attribution_k1_kernel(
         turn_b(0, 2)
         quantize_b(0, 2)
         turn_u(1)
-        block_matmul(0, 0, 0)
-        block_residual(0, 0, 0)
-        quantize_act(0, 1, 0)
-        quantize_act(0, 1, 1)
+        quantize_u(1)
         turn_b(0, 3)
-        quantize_b(0, 3)
-        turn_b(1, 0)
+        block_matmul(0, 0, 0)
         block_matmul(0, 0, 1)
-        block_residual(0, 0, 1)
-        block_matmul(0, 0, 2)
-        block_residual(0, 0, 2)
-        interleave(on_scalar, 0, 0, 0)
-        block_matmul(0, 0, 3)
-        block_residual(0, 0, 3)
+        quantize_b(0, 3)
         block_matmul(0, 1, 0)
-        block_residual(0, 1, 0)
-        quantize_b(1, 0)
-        quantize_act(1, 0, 0)
-        interleave(on_scalar, 0, 0, 1)
         block_matmul(0, 1, 1)
+        block_residual(0, 0, 0)
+        block_residual(0, 0, 1)
+        interleave(on_scalar, 0, 0, 0)
+        block_matmul(0, 0, 2)
+        block_matmul(0, 0, 3)
+        block_residual(0, 1, 0)
         block_residual(0, 1, 1)
+        interleave(on_scalar, 0, 1, 0)
         block_matmul(0, 1, 2)
-        block_residual(0, 1, 2)
         block_matmul(0, 1, 3)
+        block_residual(0, 0, 2)
+        block_residual(0, 0, 3)
+        turn_b(1, 0)
+        block_residual(0, 1, 2)
         block_residual(0, 1, 3)
+        interleave(on_vector, 0, 0, 1)
         turn_b(1, 1)
-        quantize_act(1, 0, 1)
-        interleave(on_vector, 0, 1, 0)
-        turn_b(1, 2)
-        quantize_b(1, 1)
         quantize_act(1, 1, 0)
+        quantize_act(1, 0, 0)
+        quantize_act(1, 0, 1)
+        turn_b(1, 2)
+        quantize_b(1, 0)
         turn_b(1, 3)
-        quantize_b(1, 2)
-        interleave(on_scalar, 0, 1, 1)
+        quantize_b(1, 1)
         block_matmul(1, 0, 0)
+        quantize_b(1, 2)
+        block_matmul(1, 0, 1)
         block_residual(1, 0, 0)
         quantize_b(1, 3)
-        block_matmul(1, 0, 1)
+        interleave(on_scalar, 0, 1, 1)
         block_residual(1, 0, 1)
-        quantize_act(1, 1, 1)
-        interleave(on_scalar, 1, 0, 0)
         block_matmul(1, 0, 2)
-        block_residual(1, 0, 2)
         block_matmul(1, 0, 3)
+        block_residual(1, 0, 2)
+        interleave(on_scalar, 1, 0, 0)
         block_residual(1, 0, 3)
+        quantize_act(1, 1, 1)
         block_matmul(1, 1, 0)
-        block_residual(1, 1, 0)
         block_matmul(1, 1, 1)
         block_matmul(1, 1, 2)
-        block_matmul(1, 1, 3)
         interleave(on_vector, 1, 0, 1)
         quantize_act(2, 0, 0)
         quantize_act(2, 0, 1)
+        block_residual(1, 1, 0)
         block_residual(1, 1, 1)
-        block_residual(1, 1, 2)
         interleave(on_scalar, 1, 1, 0)
-        feature_matmul(0, 0, 0)
-        feature_matmul(0, 0, 1)
-        attribute(0, 0, 0)
-        attribute(0, 0, 1)
-        store_y(0, 0)
-        round_y(on_scalar, 0, 0, 0)
-        round_y(on_scalar, 0, 0, 1)
+        block_residual(1, 1, 2)
+        block_matmul(1, 1, 3)
+        feature_matmul(0, 0, 0, 0)
+        feature_matmul(0, 0, 0, 1)
+        attribute(0, 0, 0, 0)
+        round_y(on_pool, 0, 0, 0, 0)
+        feature_matmul(0, 0, 1, 0)
+        feature_matmul(0, 0, 1, 1)
+        attribute(0, 0, 0, 1)
+        store_y(0, 0, 0, 0, 2)
+        round_y(on_pool, 0, 0, 0, 1)
+        attribute(0, 0, 1, 0)
+        round_y(on_scalar, 0, 0, 1, 0)
         block_residual(1, 1, 3)
-        feature_matmul(0, 1, 0)
-        feature_matmul(0, 1, 1)
-        attribute(0, 1, 0)
-        attribute(0, 1, 1)
-        store_y(0, 1)
-        round_y(on_scalar, 0, 1, 0)
-        interleave(on_scalar, 1, 1, 1)
-        feature_matmul(0, 2, 0)
-        feature_matmul(0, 2, 1)
-        attribute(0, 2, 0)
-        round_y(on_vector, 0, 1, 1)
+        attribute(0, 0, 1, 1)
+        store_y(0, 0, 1, 0, 2)
         quantize_act(2, 1, 0)
-        attribute(0, 2, 1)
-        store_y(0, 2)
-        round_y(on_scalar, 0, 2, 0)
-        round_y(on_scalar, 0, 2, 1)
-        feature_matmul(0, 3, 0)
-        feature_matmul(0, 3, 1)
-        turn_y(0, 0)
-        turn_y(0, 1)
-        attribute(0, 3, 0)
-        attribute(0, 3, 1)
-        store_y(0, 3)
-        round_y(on_scalar, 0, 3, 0)
-        drain_y(0, 0)
-        feature_matmul(0, 4, 0)
-        feature_matmul(0, 4, 1)
-        attribute(0, 4, 0)
-        round_y(on_vector, 0, 3, 1)
+        round_y(on_scalar, 0, 0, 1, 1)
+        feature_matmul(0, 1, 0, 0)
+        feature_matmul(0, 1, 0, 1)
+        attribute(0, 1, 0, 0)
+        interleave(on_scalar, 1, 1, 1)
+        round_y(on_pool, 0, 1, 0, 0)
+        feature_matmul(0, 1, 1, 0)
+        feature_matmul(0, 1, 1, 1)
+        turn_y(0, 0, 0)
+        turn_y(0, 0, 1)
+        drain_y(on_scalar, 0, 0, 0)
+        drain_y(on_scalar, 0, 0, 1)
+        attribute(0, 1, 0, 1)
+        store_y(0, 1, 0, 0, 2)
+        round_y(on_pool, 0, 1, 0, 1)
+        attribute(0, 1, 1, 0)
+        round_y(on_scalar, 0, 1, 1, 0)
+        attribute(0, 1, 1, 1)
+        store_y(0, 1, 1, 0, 2)
+        round_y(on_scalar, 0, 1, 1, 1)
+        feature_matmul(0, 2, 0, 0)
+        feature_matmul(0, 2, 0, 1)
+        attribute(0, 2, 0, 0)
         quantize_act(2, 1, 1)
-        attribute(0, 4, 1)
-        store_y(0, 4)
-        round_y(on_scalar, 0, 4, 0)
-        drain_y(0, 1)
-        round_y(on_scalar, 0, 4, 1)
-        feature_matmul(0, 5, 0)
-        feature_matmul(0, 5, 1)
-        turn_y(0, 2)
-        turn_y(0, 3)
-        attribute(0, 5, 0)
-        quantize_y(0, 0)
-        store_y_words(0, 0)
-        attribute(0, 5, 1)
-        store_y(0, 5)
-        round_y(on_scalar, 0, 5, 0)
-        drain_y(0, 2)
-        feature_matmul(1, 0, 0)
-        feature_matmul(1, 0, 1)
-        attribute(1, 0, 0)
-        round_y(on_vector, 0, 5, 1)
-        quantize_y(0, 1)
-        store_y_words(0, 1)
-        attribute(1, 0, 1)
-        store_y(1, 0)
-        round_y(on_scalar, 1, 0, 0)
-        drain_y(0, 3)
-        round_y(on_scalar, 1, 0, 1)
-        feature_matmul(1, 1, 0)
-        feature_matmul(1, 1, 1)
-        turn_y(0, 4)
-        turn_y(0, 5)
-        attribute(1, 1, 0)
-        quantize_y(0, 2)
-        store_y_words(0, 2)
-        attribute(1, 1, 1)
-        store_y(1, 1)
-        round_y(on_scalar, 1, 1, 0)
-        drain_y(0, 4)
-        feature_matmul(1, 2, 0)
-        feature_matmul(1, 2, 1)
-        attribute(1, 2, 0)
-        round_y(on_vector, 1, 1, 1)
-        quantize_y(0, 3)
-        store_y_words(0, 3)
-        attribute(1, 2, 1)
-        store_y(1, 2)
-        round_y(on_scalar, 1, 2, 0)
-        drain_y(0, 5)
-        round_y(on_scalar, 1, 2, 1)
-        feature_matmul(1, 3, 0)
-        feature_matmul(1, 3, 1)
-        turn_y(1, 0)
-        turn_y(1, 1)
-        attribute(1, 3, 0)
-        quantize_y(0, 4)
-        store_y_words(0, 4)
-        attribute(1, 3, 1)
-        store_y(1, 3)
-        round_y(on_scalar, 1, 3, 0)
-        drain_y(1, 0)
-        feature_matmul(1, 4, 0)
-        feature_matmul(1, 4, 1)
-        attribute(1, 4, 0)
-        round_y(on_vector, 1, 3, 1)
-        quantize_y(0, 5)
-        store_y_words(0, 5)
+        quantize_y(0, 0, 0, 2)
+        store_y_words(0, 0, 0, 2)
+        round_y(on_pool, 0, 2, 0, 0)
+        feature_matmul(0, 2, 1, 0)
+        feature_matmul(0, 2, 1, 1)
+        turn_y(0, 1, 0)
+        turn_y(0, 1, 1)
+        drain_y(on_scalar, 0, 1, 0)
+        drain_y(on_scalar, 0, 1, 1)
+        attribute(0, 2, 0, 1)
+        store_y(0, 2, 0, 0, 2)
+        round_y(on_pool, 0, 2, 0, 1)
+        attribute(0, 2, 1, 0)
+        round_y(on_scalar, 0, 2, 1, 0)
+        attribute(0, 2, 1, 1)
+        store_y(0, 2, 1, 0, 2)
+        round_y(on_scalar, 0, 2, 1, 1)
+        feature_matmul(1, 0, 0, 0)
+        feature_matmul(1, 0, 0, 1)
+        attribute(1, 0, 0, 0)
+        quantize_y(0, 1, 0, 2)
+        store_y_words(0, 1, 0, 2)
+        round_y(on_pool, 1, 0, 0, 0)
+        feature_matmul(1, 0, 1, 0)
+        feature_matmul(1, 0, 1, 1)
+        turn_y(0, 2, 0)
+        turn_y(0, 2, 1)
+        drain_y(on_scalar, 0, 2, 0)
+        drain_y(on_scalar, 0, 2, 1)
+        attribute(1, 0, 0, 1)
+        store_y(1, 0, 0, 0, 2)
+        round_y(on_pool, 1, 0, 0, 1)
+        attribute(1, 0, 1, 0)
+        round_y(on_scalar, 1, 0, 1, 0)
+        attribute(1, 0, 1, 1)
+        store_y(1, 0, 1, 0, 2)
+        round_y(on_scalar, 1, 0, 1, 1)
+        feature_matmul(1, 1, 0, 0)
+        feature_matmul(1, 1, 0, 1)
+        attribute(1, 1, 0, 0)
+        quantize_y(0, 2, 0, 2)
+        store_y_words(0, 2, 0, 2)
         store_y_scales(0)
-        attribute(1, 4, 1)
-        store_y(1, 4)
-        round_y(on_scalar, 1, 4, 0)
-        drain_y(1, 1)
-        feature_matmul(1, 5, 0)
-        feature_matmul(1, 5, 1)
-        turn_y(1, 2)
-        turn_y(1, 3)
-        attribute(1, 5, 0)
-        round_y(on_vector, 1, 4, 1)
-        quantize_y(1, 0)
-        store_y_words(1, 0)
-        attribute(1, 5, 1)
-        store_y(1, 5)
-        round_y(on_scalar, 1, 5, 0)
-        drain_y(1, 2)
-        round_y(on_vector, 1, 5, 1)
-        turn_y(1, 4)
-        turn_y(1, 5)
-        quantize_y(1, 1)
-        store_y_words(1, 1)
-        drain_y(1, 3)
-        quantize_y(1, 2)
-        store_y_words(1, 2)
-        drain_y(1, 4)
-        quantize_y(1, 3)
-        store_y_words(1, 3)
-        drain_y(1, 5)
-        quantize_y(1, 4)
-        store_y_words(1, 4)
-        quantize_y(1, 5)
-        store_y_words(1, 5)
+        round_y(on_pool, 1, 1, 0, 0)
+        feature_matmul(1, 1, 1, 0)
+        feature_matmul(1, 1, 1, 1)
+        turn_y(1, 0, 0)
+        turn_y(1, 0, 1)
+        drain_y(on_scalar, 1, 0, 0)
+        drain_y(on_scalar, 1, 0, 1)
+        attribute(1, 1, 0, 1)
+        store_y(1, 1, 0, 0, 2)
+        round_y(on_pool, 1, 1, 0, 1)
+        attribute(1, 1, 1, 0)
+        round_y(on_scalar, 1, 1, 1, 0)
+        attribute(1, 1, 1, 1)
+        store_y(1, 1, 1, 0, 2)
+        round_y(on_scalar, 1, 1, 1, 1)
+        feature_matmul(1, 2, 0, 0)
+        feature_matmul(1, 2, 0, 1)
+        attribute(1, 2, 0, 0)
+        quantize_y(1, 0, 0, 2)
+        store_y_words(1, 0, 0, 2)
+        round_y(on_pool, 1, 2, 0, 0)
+        feature_matmul(1, 2, 1, 0)
+        feature_matmul(1, 2, 1, 1)
+        turn_y(1, 1, 0)
+        turn_y(1, 1, 1)
+        drain_y(on_scalar, 1, 1, 0)
+        drain_y(on_scalar, 1, 1, 1)
+        attribute(1, 2, 0, 1)
+        store_y(1, 2, 0, 0, 2)
+        round_y(on_pool, 1, 2, 0, 1)
+        attribute(1, 2, 1, 0)
+        store_y(1, 2, 1, 0, 1)
+        attribute(1, 2, 1, 1)
+        store_y(1, 2, 1, 1, 2)
+        round_y(on_vector, 1, 2, 1, 0)
+        round_y(on_vector, 1, 2, 1, 1)
+        turn_y(1, 2, 0)
+        drain_y(on_scalar, 1, 2, 0)
+        turn_y(1, 2, 1)
+        quantize_y(1, 1, 0, 2)
+        store_y_words(1, 1, 0, 2)
+        drain_y(on_vector, 1, 2, 1)
+        quantize_y(1, 2, 0, 1)
+        store_y_words(1, 2, 0, 1)
+        quantize_y(1, 2, 1, 2)
+        store_y_words(1, 2, 1, 2)
         store_y_scales(1)

@@ -35,7 +35,7 @@ def tile_sae_feature_attribution_k1_kernel(
         ctx.enter_context(tc.manual_schedule())
 
         def kept(name, shape, dtype):
-            return keep.tile(shape, dtype, name=name, align_bytes=64)
+            return keep.tile(shape, dtype, name=name, align_bytes=256)
 
         def new_bank():
             return psum.tile([P, KP], F32, name="bank", tag="bank")
@@ -44,15 +44,15 @@ def tile_sae_feature_attribution_k1_kernel(
         gains = [kept("gain%d" % s, [P, GD, 4], BF16) for s in range(2)]
         u_raw = [kept("u_raw%d" % j, [P, D], BF16) for j in range(4)]
         b_raw = [[kept("b_raw%d_%d" % (s, q), [P, 2, D], BF16) for q in range(4)] for s in range(2)]
-        b_codes = [[kept("b_codes%d_%d" % (s, q), [P, 2, GD, P], U32) for q in range(4)] for s in range(2)]
-        b_scales = [[kept("b_scales%d_%d" % (s, q), [P, 2, GD, P], U8) for q in range(4)] for s in range(2)]
+        b_codes = kept("b_codes", [P, 2, 4, 2 * GD * P], U32)
+        b_scales = kept("b_scales", [P, 2, 4, 2 * GD * P], U8)
         c_words = [kept("c_words%d" % c, [P, GD, 2 * width], U8) for c, width in enumerate((CW, F - CW))]
         c_scales = kept("c_scales", [P, GD, F], U8)
         z_first = [kept("z_first%d" % c, [P, 2, width], BF16) for c, width in enumerate((CW, F - CW))]
         z_second = [kept("z_second%d" % i, [P, F], BF16) for i in range(2)]
         act = [[kept("act%d_%d" % (s, h), [P, GD, HT, 4], BF16) for h in range(2)] for s in range(3)]
-        act_codes = [[kept("act_codes%d_%d" % (s, h), [P, GD, HT], U32) for h in range(2)] for s in range(3)]
-        act_scales = [[kept("act_scales%d_%d" % (s, h), [P, GD, HT], U8) for h in range(2)] for s in range(3)]
+        act_codes = kept("act_codes", [P, 3, 2, GD * HT], U32)
+        act_scales = kept("act_scales", [P, 3, 2, GD * HT], U8)
         rows = [[kept("rows%d_%d" % (s, h), [P, GD, 4, HT], (F32, BF16)[s]) for h in range(2)] for s in range(2)]
         y_scales = [kept("y_scales%d" % h, [P, GF, HT], U8) for h in range(2)]
 
@@ -105,24 +105,25 @@ def tile_sae_feature_attribution_k1_kernel(
         b_turned = {}
 
         def turn_b(s, q):
-            b_turned[s, q] = stage.tile([P, 2, GD, P, 4], BF16, name="b_turned", bufs=4, align_bytes=64)
+            b_turned[s, q] = stage.tile([P, 2, GD, P, 4], BF16, name="b_turned", align_bytes=256)
             for i in range(2):
                 turn(b_raw[s][q][:, i, :], b_turned[s, q][:, i, :, :, :])
 
         def quantize_b(s, q):
             quantize(
-                b_codes[s][q][:].rearrange("p i g r -> p (i g r)"),
-                b_scales[s][q][:].rearrange("p i g r -> p (i g r)"),
+                b_codes[:, s, q, :],
+                b_scales[:, s, q, :],
                 b_turned[s, q][:].rearrange("p i g r t -> p (i g r t)"),
             )
 
         def quantize_act(s, h, g):
-            quantize(act_codes[s][h][:, g, :], act_scales[s][h][:, g, :], act[s][h][:, g, :, :].rearrange("p n t -> p (n t)"))
+            cols = slice(g * HT, (g + 1) * HT)
+            quantize(act_codes[:, s, h, cols], act_scales[:, s, h, cols], act[s][h][:, g, :, :].rearrange("p n t -> p (n t)"))
 
         def quantize_u(h):
             quantize(
-                act_codes[0][h][:].rearrange("p g n -> p (g n)"),
-                act_scales[0][h][:].rearrange("p g n -> p (g n)"),
+                act_codes[:, 0, h, :],
+                act_scales[:, 0, h, :],
                 act[0][h][:].rearrange("p g n t -> p (g n t)"),
             )
 
@@ -132,12 +133,14 @@ def tile_sae_feature_attribution_k1_kernel(
             banks[s, h, q] = new_bank()
             for i in range(2):
                 for g in range(GD):
+                    chans = slice((i * GD + g) * P, (i * GD + g + 1) * P)
+                    toks = slice(g * HT, (g + 1) * HT)
                     nc.tensor.matmul_mx(
                         out=banks[s, h, q][:, i * HT : (i + 1) * HT],
-                        lhsT=b_codes[s][q][:, i, g, :].bitcast(FP8X4),
-                        lhsT_scale=b_scales[s][q][:, i, g, :],
-                        rhs=act_codes[s][h][:, g, :].bitcast(FP8X4),
-                        rhs_scale=act_scales[s][h][:, g, :],
+                        lhsT=b_codes[:, s, q, chans].bitcast(FP8X4),
+                        lhsT_scale=b_scales[:, s, q, chans],
+                        rhs=act_codes[:, s, h, toks].bitcast(FP8X4),
+                        rhs_scale=act_scales[:, s, h, toks],
                         start=(g == 0),
                         stop=(g == GD - 1),
                     )
@@ -167,10 +170,11 @@ def tile_sae_feature_attribution_k1_kernel(
             at = f0 - c * CW
             y_bank[h, k, i, j] = new_bank()
             for g in range(GD):
+                toks = slice(g * HT + i * P, g * HT + (i + 1) * P)
                 nc.tensor.matmul_mx(
                     out=y_bank[h, k, i, j][:],
-                    lhsT=act_codes[2][h][:, g, i * P : (i + 1) * P].bitcast(FP8X4),
-                    lhsT_scale=act_scales[2][h][:, g, i * P : (i + 1) * P],
+                    lhsT=act_codes[:, 2, h, toks].bitcast(FP8X4),
+                    lhsT_scale=act_scales[:, 2, h, toks],
                     rhs=c_words[c][:, g, 2 * at : 2 * (at + KP)].bitcast(FP4X4),
                     rhs_scale=c_scales[:, g, f0 : f0 + KP],
                     start=(g == 0),
@@ -182,7 +186,7 @@ def tile_sae_feature_attribution_k1_kernel(
             c = min(k, 1)
             at = f0 - c * CW
             if j == 0:
-                y_sb[h, k, i] = stage.tile([P, 2, KP], F32, name="y_sb", bufs=5, align_bytes=64)
+                y_sb[h, k, i] = stage.tile([P, 2, KP], F32, name="y_sb", bufs=5, align_bytes=256)
             nc.vector.scalar_tensor_tensor(
                 out=y_sb[h, k, i][:, j, :],
                 in0=z_first[c][:, i, at : at + KP] if h == 0 else z_second[i][:, f0 : f0 + KP],
@@ -198,7 +202,7 @@ def tile_sae_feature_attribution_k1_kernel(
             nc.sync.dma_start(out=out_0[r0 : r0 + P, f0 + j0 * KP : f0 + j1 * KP], in_=src)
 
         def round_y(copy, h, k, i, j):
-            y_bf[h, k, i, j] = stage.tile([P, 2, P, 2], BF16, name="y_bf", bufs=8, align_bytes=64)
+            y_bf[h, k, i, j] = stage.tile([P, 2, P, 2], BF16, name="y_bf", bufs=8, align_bytes=256)
             copy(out=y_bf[h, k, i, j][:], in_=y_sb[h, k, i][:, j, :].rearrange("p (m u e) -> p u m e", u=2, e=2))
 
         def turn_y(h, k, i):
@@ -211,13 +215,13 @@ def tile_sae_feature_attribution_k1_kernel(
 
         def drain_y(copy, h, k, i):
             if i == 0:
-                y_turned[h, k] = stage.tile([P, 2, 2, P, 4], BF16, name="y_turned", align_bytes=64)
+                y_turned[h, k] = stage.tile([P, 2, 2, P, 4], BF16, name="y_turned", align_bytes=256)
             src = y_bank[h, k, i][:].rearrange("p (j u r) -> p j r u", j=2, u=2)
             copy(out=y_turned[h, k][:, :, i, :, :].bitcast(F32), in_=src)
 
         def quantize_y(h, k, j0, j1):
             if j0 == 0:
-                y_codes[h, k] = stage.tile([P, 2, HT], U32, name="y_codes", align_bytes=64)
+                y_codes[h, k] = stage.tile([P, 2, HT], U32, name="y_codes", align_bytes=256)
             quantize(
                 y_codes[h, k][:, j0:j1, :].rearrange("p j m -> p (j m)"),
                 y_scales[h][:, 2 * k + j0 : 2 * k + j1, :].rearrange("p j m -> p (j m)"),
@@ -307,10 +311,10 @@ def tile_sae_feature_attribution_k1_kernel(
         block_residual(1, 0, 1)
         block_matmul(1, 0, 2)
         block_matmul(1, 0, 3)
+        quantize_act(1, 1, 1)
         block_residual(1, 0, 2)
         interleave(on_scalar, 1, 0, 0)
         block_residual(1, 0, 3)
-        quantize_act(1, 1, 1)
         block_matmul(1, 1, 0)
         block_matmul(1, 1, 1)
         block_matmul(1, 1, 2)

@@ -271,61 +271,63 @@ def tile_sae_feature_attribution_k1_kernel(
         turn_b(0, 2)
         quantize_b(0, 2)
         turn_u(1)
+        block_matmul(0, 0, 0)
         quantize_u(1)
         turn_b(0, 3)
-        block_matmul(0, 0, 0)
+        block_residual(0, 0, 0)
         block_matmul(0, 0, 1)
-        quantize_b(0, 3)
         block_matmul(0, 1, 0)
         block_matmul(0, 1, 1)
-        block_residual(0, 0, 0)
+        block_matmul(0, 1, 2)
         block_residual(0, 0, 1)
         interleave(on_scalar, 0, 0, 0)
-        block_matmul(0, 0, 2)
-        block_matmul(0, 0, 3)
+        quantize_b(0, 3)
         block_residual(0, 1, 0)
+        turn_b(1, 0)
         block_residual(0, 1, 1)
         interleave(on_scalar, 0, 1, 0)
-        block_matmul(0, 1, 2)
+        block_residual(0, 1, 2)
+        quantize_act(1, 0, 0)
+        block_matmul(0, 0, 2)
+        block_matmul(0, 0, 3)
         block_matmul(0, 1, 3)
         block_residual(0, 0, 2)
         block_residual(0, 0, 3)
-        turn_b(1, 0)
-        block_residual(0, 1, 2)
         block_residual(0, 1, 3)
-        interleave(on_vector, 0, 0, 1)
         turn_b(1, 1)
-        quantize_act(1, 1, 0)
-        quantize_act(1, 0, 0)
-        quantize_act(1, 0, 1)
+        interleave(on_vector, 0, 0, 1)
         turn_b(1, 2)
-        quantize_b(1, 0)
         turn_b(1, 3)
+        quantize_b(1, 0)
+        quantize_act(1, 0, 1)
         quantize_b(1, 1)
-        block_matmul(1, 0, 0)
+        quantize_act(1, 1, 0)
+        interleave(on_scalar, 0, 1, 1)
         quantize_b(1, 2)
+        block_matmul(1, 0, 0)
         block_matmul(1, 0, 1)
+        block_matmul(1, 0, 2)
         block_residual(1, 0, 0)
         quantize_b(1, 3)
-        interleave(on_scalar, 0, 1, 1)
         block_residual(1, 0, 1)
-        block_matmul(1, 0, 2)
+        interleave(on_scalar, 1, 0, 0)
+        block_residual(1, 0, 2)
         block_matmul(1, 0, 3)
         quantize_act(1, 1, 1)
-        block_residual(1, 0, 2)
-        interleave(on_scalar, 1, 0, 0)
         block_residual(1, 0, 3)
+        interleave(on_scalar, 1, 0, 1)
         block_matmul(1, 1, 0)
         block_matmul(1, 1, 1)
         block_matmul(1, 1, 2)
-        interleave(on_vector, 1, 0, 1)
+        block_matmul(1, 1, 3)
         quantize_act(2, 0, 0)
-        quantize_act(2, 0, 1)
         block_residual(1, 1, 0)
         block_residual(1, 1, 1)
         interleave(on_scalar, 1, 1, 0)
+        quantize_act(2, 0, 1)
         block_residual(1, 1, 2)
-        block_matmul(1, 1, 3)
+        block_residual(1, 1, 3)
+        interleave(on_scalar, 1, 1, 1)
         feature_matmul(0, 0, 0, 0)
         feature_matmul(0, 0, 0, 1)
         attribute(0, 0, 0, 0)
@@ -337,15 +339,13 @@ def tile_sae_feature_attribution_k1_kernel(
         round_y(on_pool, 0, 0, 0, 1)
         attribute(0, 0, 1, 0)
         round_y(on_scalar, 0, 0, 1, 0)
-        block_residual(1, 1, 3)
         attribute(0, 0, 1, 1)
         store_y(0, 0, 1, 0, 2)
-        quantize_act(2, 1, 0)
         round_y(on_scalar, 0, 0, 1, 1)
         feature_matmul(0, 1, 0, 0)
         feature_matmul(0, 1, 0, 1)
         attribute(0, 1, 0, 0)
-        interleave(on_scalar, 1, 1, 1)
+        quantize_act(2, 1, 0)
         round_y(on_pool, 0, 1, 0, 0)
         feature_matmul(0, 1, 1, 0)
         feature_matmul(0, 1, 1, 1)
@@ -426,8 +426,6 @@ def tile_sae_feature_attribution_k1_kernel(
         feature_matmul(1, 2, 0, 0)
         feature_matmul(1, 2, 0, 1)
         attribute(1, 2, 0, 0)
-        quantize_y(1, 0, 0, 2)
-        store_y_words(1, 0, 0, 2)
         round_y(on_pool, 1, 2, 0, 0)
         feature_matmul(1, 2, 1, 0)
         feature_matmul(1, 2, 1, 1)
@@ -445,11 +443,13 @@ def tile_sae_feature_attribution_k1_kernel(
         round_y(on_vector, 1, 2, 1, 0)
         round_y(on_vector, 1, 2, 1, 1)
         turn_y(1, 2, 0)
-        drain_y(on_scalar, 1, 2, 0)
         turn_y(1, 2, 1)
+        drain_y(on_scalar, 1, 2, 0)
+        drain_y(on_scalar, 1, 2, 1)
+        quantize_y(1, 0, 0, 2)
+        store_y_words(1, 0, 0, 2)
         quantize_y(1, 1, 0, 2)
         store_y_words(1, 1, 0, 2)
-        drain_y(on_vector, 1, 2, 1)
         quantize_y(1, 2, 0, 1)
         store_y_words(1, 2, 0, 1)
         quantize_y(1, 2, 1, 2)

@@ -160,7 +160,10 @@ def tile_sae_feature_attribution_k1_kernel(
                 )
 
         def interleave(copy, s, h, g):
-            copy(out=act[s + 1][h][:, g, :, :], in_=rows[s][h][:, g, :, :].rearrange("p t n -> p n t"))
+            copy(
+                out=act[s + 1][h][:, g, :, :].rearrange("p (c i) t -> p c t i", i=4),
+                in_=rows[s][h][:, g, :, :].rearrange("p t (c i) -> p c t i", i=4),
+            )
 
         y_sb, y_bf, y_turned, y_bank, y_codes = {}, {}, {}, {}, {}
 

from contextlib import ExitStack

import concourse.mybir as mybir
from concourse.masks import make_identity

T, D, F = 512, 1024, 3072
FLOPS = 2 * T * D * (2 * D + F)

F32 = mybir.dt.float32
BF16 = mybir.dt.bfloat16
U32 = mybir.dt.uint32
I32 = mybir.dt.int32
U8 = mybir.dt.uint8
FP8X4 = mybir.dt.float8_e4m3fn_x4
FP4X4 = mybir.dt.float4_e2m1fn_x4
ALU = mybir.AluOpType

P = 128
KP = 512
GD = D // KP
GF = F // KP
HT = T // 2
CW = 1024
NC = F // CW


def tile_sae_feature_attribution_k1_kernel(
    tc, upstream, block2, gain2, block1, gain1, dec_words, dec_scales, z, out_0, out_1, out_2
):
    nc = tc.nc
    with ExitStack() as ctx:
        keep = ctx.enter_context(tc.tile_pool(name="keep", bufs=1))
        stage = ctx.enter_context(tc.tile_pool(name="stage", bufs=3))
        psum = ctx.enter_context(tc.psum_pool(name="psum", bufs=8))
        ctx.enter_context(tc.manual_schedule())

        def kept(name, shape, dtype):
            return keep.tile(shape, dtype, name=name, align_bytes=256)

        def new_bank():
            return psum.tile([P, KP], F32, name="bank", tag="bank")

        ident = kept("ident", [P, P], F32)
        gains = [kept("gain%d" % s, [P, GD, 4], BF16) for s in range(2)]
        u_raw = [kept("u_raw%d" % j, [P, D], BF16) for j in range(4)]
        b_raw = [[kept("b_raw%d_%d" % (s, q), [P, 2, D], BF16) for q in range(4)] for s in range(2)]
        b_codes = kept("b_codes", [P, 2, 4, 2 * GD * P], U32)
        b_scales = kept("b_scales", [P, 2, 4, 2 * GD * P], U8)
        c_words = [kept("c_words%d" % c, [P, GD, 2 * width], U8) for c, width in enumerate((CW, F - CW))]
        c_scales = kept("c_scales", [P, GD, F], U8)
        z_first = [kept("z_first%d" % c, [P, 2, width], BF16) for c, width in enumerate((CW, F - CW))]
        z_second = [kept("z_second%d" % i, [P, F], BF16) for i in range(2)]
        act = [[kept("act%d_%d" % (s, h), [P, GD, HT, 4], BF16) for h in range(2)] for s in range(3)]
        act_codes = kept("act_codes", [P, 3, 2, GD * HT], U32)
        act_scales = kept("act_scales", [P, 3, 2, GD * HT], U8)
        rows = [[kept("rows%d_%d" % (s, h), [P, GD, 4, HT], (F32, BF16)[s]) for h in range(2)] for s in range(2)]
        y_scales = [kept("y_scales%d" % h, [P, GF, HT], U8) for h in range(2)]

        nc.vector.memset(c_scales[:].rearrange("p g n -> p (g n)").bitcast(U32), 0)
        make_identity(nc, ident[:])
        for s, gain in enumerate((gain2, gain1)):
            nc.scalar.dma_start(out=gains[s][:], in_=gain.rearrange("(g p t) -> p g t", g=GD, t=4))

        def load_u(j):
            nc.sync.dma_start(out=u_raw[j][:], in_=upstream[j * P : (j + 1) * P, :])

        def load_b(s, q):
            g, pair = divmod(q, 2)
            src = (block2, block1)[s][g * KP : (g + 1) * KP, :].rearrange("(m t) k -> m t k", t=4)
            nc.sync.dma_start(out=b_raw[s][q][:], in_=src[:, 2 * pair : 2 * pair + 2, :])

        def load_c(c):
            cols = (slice(0, 2 * CW), slice(2 * CW, 2 * F))[c]
            src = dec_words.rearrange("g p b -> p g b")[:, :, cols]
            nc.sync.dma_start(out=c_words[c][:].bitcast(I32), in_=src.bitcast(I32))

        def load_z(h, c):
            if h == 0:
                cols = (slice(0, CW), slice(CW, F))[c]
                nc.sync.dma_start(out=z_first[c][:], in_=z[:HT, cols].rearrange("(i p) f -> p i f", i=2))
            else:
                nc.sync.dma_start(out=z_second[c][:], in_=z[HT + c * P : HT + (c + 1) * P, :])

        def load_c_scales():
            for quad in range(4):
                src = dec_scales[:, 4 * quad : 4 * quad + 4, :].rearrange("g r n -> r g n")
                nc.sync.dma_start(out=c_scales[32 * quad : 32 * quad + 4, :, :].bitcast(I32), in_=src.bitcast(I32))

        def turn(raw, dest):
            words = raw.bitcast(F32)
            bank = new_bank()
            for g in range(GD):
                for u in range(2):
                    at = (2 * g + u) * P
                    nc.tensor.transpose(bank[:, at : at + P], words[:, 2 * P * g + u : 2 * P * (g + 1) : 2], ident[:])
            nc.scalar.copy(out=dest.bitcast(F32), in_=bank[:].rearrange("p (g u r) -> p g r u", g=GD, u=2))

        def quantize(codes, scales, src):
            nc.vector.quantize_mx(out=codes.bitcast(FP8X4), scales=scales, in_=src)

        def turn_u(h):
            for i in range(2):
                turn(u_raw[2 * h + i][:], act[0][h][:, :, i * P : (i + 1) * P, :])

        b_turned = {}

        def turn_b(s, q):
            b_turned[s, q] = stage.tile([P, 2, GD, P, 4], BF16, name="b_turned", align_bytes=256)
            for i in range(2):
                turn(b_raw[s][q][:, i, :], b_turned[s, q][:, i, :, :, :])

        def quantize_b(s, q):
            quantize(
                b_codes[:, s, q, :],
                b_scales[:, s, q, :],
                b_turned[s, q][:].rearrange("p i g r t -> p (i g r t)"),
            )

        def quantize_act(s, h, g):
            cols = slice(g * HT, (g + 1) * HT)
            quantize(act_codes[:, s, h, cols], act_scales[:, s, h, cols], act[s][h][:, g, :, :].rearrange("p n t -> p (n t)"))

        def quantize_u(h):
            quantize(
                act_codes[:, 0, h, :],
                act_scales[:, 0, h, :],
                act[0][h][:].rearrange("p g n t -> p (g n t)"),
            )

        banks = {}

        def block_matmul(s, h, q):
            banks[s, h, q] = new_bank()
            for i in range(2):
                for g in range(GD):
                    chans = slice((i * GD + g) * P, (i * GD + g + 1) * P)
                    toks = slice(g * HT, (g + 1) * HT)
                    nc.tensor.matmul_mx(
                        out=banks[s, h, q][:, i * HT : (i + 1) * HT],
                        lhsT=b_codes[:, s, q, chans].bitcast(FP8X4),
                        lhsT_scale=b_scales[:, s, q, chans],
                        rhs=act_codes[:, s, h, toks].bitcast(FP8X4),
                        rhs_scale=act_scales[:, s, h, toks],
                        start=(g == 0),
                        stop=(g == GD - 1),
                    )

        def block_residual(s, h, q):
            g, pair = divmod(q, 2)
            for i in range(2):
                t = 2 * pair + i
                src = act[0][h][:, g, :, t] if s == 0 else rows[0][h][:, g, t, :]
                nc.vector.scalar_tensor_tensor(
                    out=rows[s][h][:, g, t, :],
                    in0=src,
                    scalar=gains[s][:, g, t : t + 1],
                    in1=banks[s, h, q][:, i * HT : (i + 1) * HT],
                    op0=ALU.mult,
                    op1=ALU.add,
                )

        def interleave(copy, s, h, g):
            copy(
                out=act[s + 1][h][:, g, :, :].rearrange("p (c i) t -> p c t i", i=4),
                in_=rows[s][h][:, g, :, :].rearrange("p t (c i) -> p c t i", i=4),
            )

        y_sb, y_bf, y_turned, y_bank, y_codes = {}, {}, {}, {}, {}

        def feature_matmul(h, k, i, j):
            f0 = k * CW + j * KP
            c = min(k, 1)
            at = f0 - c * CW
            y_bank[h, k, i, j] = new_bank()
            for g in range(GD):
                toks = slice(g * HT + i * P, g * HT + (i + 1) * P)
                nc.tensor.matmul_mx(
                    out=y_bank[h, k, i, j][:],
                    lhsT=act_codes[:, 2, h, toks].bitcast(FP8X4),
                    lhsT_scale=act_scales[:, 2, h, toks],
                    rhs=c_words[c][:, g, 2 * at : 2 * (at + KP)].bitcast(FP4X4),
                    rhs_scale=c_scales[:, g, f0 : f0 + KP],
                    start=(g == 0),
                    stop=(g == GD - 1),
                )

        def attribute(h, k, i, j):
            f0 = k * CW + j * KP
            c = min(k, 1)
            at = f0 - c * CW
            if j == 0:
                y_sb[h, k, i] = stage.tile([P, 2, KP], F32, name="y_sb", bufs=5, align_bytes=256)
            nc.vector.scalar_tensor_tensor(
                out=y_sb[h, k, i][:, j, :],
                in0=z_first[c][:, i, at : at + KP] if h == 0 else z_second[i][:, f0 : f0 + KP],
                scalar=0.0,
                in1=y_bank[h, k, i, j][:],
                op0=ALU.max,
                op1=ALU.mult,
            )

        def store_y(h, k, i, j0, j1):
            r0, f0 = h * HT + i * P, k * CW
            src = y_sb[h, k, i][:, j0:j1, :].rearrange("p j f -> p (j f)")
            nc.sync.dma_start(out=out_0[r0 : r0 + P, f0 + j0 * KP : f0 + j1 * KP], in_=src)

        def round_y(copy, h, k, i, j):
            y_bf[h, k, i, j] = stage.tile([P, 2, P, 2], BF16, name="y_bf", bufs=8, align_bytes=256)
            copy(out=y_bf[h, k, i, j][:], in_=y_sb[h, k, i][:, j, :].rearrange("p (m u e) -> p u m e", u=2, e=2))

        def turn_y(h, k, i):
            y_bank[h, k, i] = new_bank()
            for j in range(2):
                words = y_bf[h, k, i, j][:].rearrange("p u m e -> p (u m e)").bitcast(F32)
                for u in range(2):
                    at = (2 * j + u) * P
                    nc.tensor.transpose(y_bank[h, k, i][:, at : at + P], words[:, u * P : (u + 1) * P], ident[:])

        def drain_y(copy, h, k, i):
            if i == 0:
                y_turned[h, k] = stage.tile([P, 2, 2, P, 4], BF16, name="y_turned", align_bytes=256)
            src = y_bank[h, k, i][:].rearrange("p (j u r) -> p j r u", j=2, u=2)
            copy(out=y_turned[h, k][:, :, i, :, :].bitcast(F32), in_=src)

        def quantize_y(h, k, j0, j1):
            if j0 == 0:
                y_codes[h, k] = stage.tile([P, 2, HT], U32, name="y_codes", align_bytes=256)
            quantize(
                y_codes[h, k][:, j0:j1, :].rearrange("p j m -> p (j m)"),
                y_scales[h][:, 2 * k + j0 : 2 * k + j1, :].rearrange("p j m -> p (j m)"),
                y_turned[h, k][:, j0:j1, :, :, :].rearrange("p j i r t -> p (j i r t)"),
            )

        def store_y_words(h, k, j0, j1):
            dst = out_1[2 * k + j0 : 2 * k + j1].rearrange("g p m t -> p g (m t)")[:, :, 4 * HT * h : 4 * HT * (h + 1)]
            nc.sync.dma_start(out=dst.bitcast(I32), in_=y_codes[h, k][:, j0:j1, :].bitcast(I32))

        def store_y_scales(h):
            for quad in range(4):
                dst = out_2[:, 4 * quad : 4 * quad + 4, h * HT : (h + 1) * HT].rearrange("g r m -> r g m")
                queue = nc.scalar if h == 1 and quad >= 2 else nc.sync
                queue.dma_start(out=dst.bitcast(I32), in_=y_scales[h][32 * quad : 32 * quad + 4, :, :].bitcast(I32))

        on_scalar, on_vector = nc.scalar.copy, nc.vector.tensor_copy

        def on_pool(out, in_):
            nc.gpsimd.tensor_scalar(out=out, in0=in_, scalar1=1.0, scalar2=1.0, op0=ALU.mult, op1=ALU.mult)

        load_u(0)
        load_u(1)
        load_b(0, 0)
        load_b(0, 1)
        load_b(0, 2)
        load_u(2)
        load_u(3)
        load_b(0, 3)
        load_b(1, 0)
        load_b(1, 1)
        load_b(1, 2)
        load_b(1, 3)
        load_c_scales()
        load_c(0)
        load_z(0, 0)
        load_c(1)
        load_z(0, 1)
        load_z(1, 0)
        load_z(1, 1)
        turn_u(0)
        quantize_u(0)
        turn_b(0, 0)
        quantize_b(0, 0)
        turn_b(0, 1)
        quantize_b(0, 1)
        turn_b(0, 2)
        quantize_b(0, 2)
        turn_u(1)
        block_matmul(0, 0, 0)
        quantize_u(1)
        turn_b(0, 3)
        block_residual(0, 0, 0)
        block_matmul(0, 0, 1)
        block_matmul(0, 1, 0)
        block_matmul(0, 1, 1)
        block_matmul(0, 1, 2)
        block_residual(0, 0, 1)
        interleave(on_scalar, 0, 0, 0)
        quantize_b(0, 3)
        block_residual(0, 1, 0)
        turn_b(1, 0)
        block_residual(0, 1, 1)
        interleave(on_scalar, 0, 1, 0)
        block_residual(0, 1, 2)
        quantize_act(1, 0, 0)
        block_matmul(0, 0, 2)
        block_matmul(0, 0, 3)
        block_matmul(0, 1, 3)
        block_residual(0, 0, 2)
        block_residual(0, 0, 3)
        block_residual(0, 1, 3)
        turn_b(1, 1)
        interleave(on_vector, 0, 0, 1)
        turn_b(1, 2)
        turn_b(1, 3)
        quantize_b(1, 0)
        quantize_act(1, 0, 1)
        quantize_b(1, 1)
        quantize_act(1, 1, 0)
        interleave(on_scalar, 0, 1, 1)
        quantize_b(1, 2)
        block_matmul(1, 0, 0)
        block_matmul(1, 0, 1)
        block_matmul(1, 0, 2)
        block_residual(1, 0, 0)
        quantize_b(1, 3)
        block_residual(1, 0, 1)
        interleave(on_scalar, 1, 0, 0)
        block_residual(1, 0, 2)
        block_matmul(1, 0, 3)
        quantize_act(1, 1, 1)
        block_residual(1, 0, 3)
        interleave(on_scalar, 1, 0, 1)
        block_matmul(1, 1, 0)
        block_matmul(1, 1, 1)
        block_matmul(1, 1, 2)
        block_matmul(1, 1, 3)
        quantize_act(2, 0, 0)
        block_residual(1, 1, 0)
        block_residual(1, 1, 1)
        interleave(on_scalar, 1, 1, 0)
        quantize_act(2, 0, 1)
        block_residual(1, 1, 2)
        block_residual(1, 1, 3)
        interleave(on_scalar, 1, 1, 1)
        feature_matmul(0, 0, 0, 0)
        feature_matmul(0, 0, 0, 1)
        attribute(0, 0, 0, 0)
        round_y(on_pool, 0, 0, 0, 0)
        feature_matmul(0, 0, 1, 0)
        feature_matmul(0, 0, 1, 1)
        attribute(0, 0, 0, 1)
        store_y(0, 0, 0, 0, 2)
        round_y(on_pool, 0, 0, 0, 1)
        attribute(0, 0, 1, 0)
        round_y(on_scalar, 0, 0, 1, 0)
        attribute(0, 0, 1, 1)
        store_y(0, 0, 1, 0, 2)
        round_y(on_scalar, 0, 0, 1, 1)
        feature_matmul(0, 1, 0, 0)
        feature_matmul(0, 1, 0, 1)
        attribute(0, 1, 0, 0)
        quantize_act(2, 1, 0)
        round_y(on_pool, 0, 1, 0, 0)
        feature_matmul(0, 1, 1, 0)
        feature_matmul(0, 1, 1, 1)
        turn_y(0, 0, 0)
        turn_y(0, 0, 1)
        drain_y(on_scalar, 0, 0, 0)
        drain_y(on_scalar, 0, 0, 1)
        attribute(0, 1, 0, 1)
        store_y(0, 1, 0, 0, 2)
        round_y(on_pool, 0, 1, 0, 1)
        attribute(0, 1, 1, 0)
        round_y(on_scalar, 0, 1, 1, 0)
        attribute(0, 1, 1, 1)
        store_y(0, 1, 1, 0, 2)
        round_y(on_scalar, 0, 1, 1, 1)
        feature_matmul(0, 2, 0, 0)
        feature_matmul(0, 2, 0, 1)
        attribute(0, 2, 0, 0)
        quantize_act(2, 1, 1)
        quantize_y(0, 0, 0, 2)
        store_y_words(0, 0, 0, 2)
        round_y(on_pool, 0, 2, 0, 0)
        feature_matmul(0, 2, 1, 0)
        feature_matmul(0, 2, 1, 1)
        turn_y(0, 1, 0)
        turn_y(0, 1, 1)
        drain_y(on_scalar, 0, 1, 0)
        drain_y(on_scalar, 0, 1, 1)
        attribute(0, 2, 0, 1)
        store_y(0, 2, 0, 0, 2)
        round_y(on_pool, 0, 2, 0, 1)
        attribute(0, 2, 1, 0)
        round_y(on_scalar, 0, 2, 1, 0)
        attribute(0, 2, 1, 1)
        store_y(0, 2, 1, 0, 2)
        round_y(on_scalar, 0, 2, 1, 1)
        feature_matmul(1, 0, 0, 0)
        feature_matmul(1, 0, 0, 1)
        attribute(1, 0, 0, 0)
        quantize_y(0, 1, 0, 2)
        store_y_words(0, 1, 0, 2)
        round_y(on_pool, 1, 0, 0, 0)
        feature_matmul(1, 0, 1, 0)
        feature_matmul(1, 0, 1, 1)
        turn_y(0, 2, 0)
        turn_y(0, 2, 1)
        drain_y(on_scalar, 0, 2, 0)
        drain_y(on_scalar, 0, 2, 1)
        attribute(1, 0, 0, 1)
        store_y(1, 0, 0, 0, 2)
        round_y(on_pool, 1, 0, 0, 1)
        attribute(1, 0, 1, 0)
        round_y(on_scalar, 1, 0, 1, 0)
        attribute(1, 0, 1, 1)
        store_y(1, 0, 1, 0, 2)
        round_y(on_scalar, 1, 0, 1, 1)
        feature_matmul(1, 1, 0, 0)
        feature_matmul(1, 1, 0, 1)
        attribute(1, 1, 0, 0)
        quantize_y(0, 2, 0, 2)
        store_y_words(0, 2, 0, 2)
        store_y_scales(0)
        round_y(on_pool, 1, 1, 0, 0)
        feature_matmul(1, 1, 1, 0)
        feature_matmul(1, 1, 1, 1)
        turn_y(1, 0, 0)
        turn_y(1, 0, 1)
        drain_y(on_scalar, 1, 0, 0)
        drain_y(on_scalar, 1, 0, 1)
        attribute(1, 1, 0, 1)
        store_y(1, 1, 0, 0, 2)
        round_y(on_pool, 1, 1, 0, 1)
        attribute(1, 1, 1, 0)
        round_y(on_scalar, 1, 1, 1, 0)
        attribute(1, 1, 1, 1)
        store_y(1, 1, 1, 0, 2)
        round_y(on_scalar, 1, 1, 1, 1)
        feature_matmul(1, 2, 0, 0)
        feature_matmul(1, 2, 0, 1)
        attribute(1, 2, 0, 0)
        round_y(on_pool, 1, 2, 0, 0)
        feature_matmul(1, 2, 1, 0)
        feature_matmul(1, 2, 1, 1)
        turn_y(1, 1, 0)
        turn_y(1, 1, 1)
        drain_y(on_scalar, 1, 1, 0)
        drain_y(on_scalar, 1, 1, 1)
        attribute(1, 2, 0, 1)
        store_y(1, 2, 0, 0, 2)
        round_y(on_pool, 1, 2, 0, 1)
        attribute(1, 2, 1, 0)
        store_y(1, 2, 1, 0, 1)
        attribute(1, 2, 1, 1)
        store_y(1, 2, 1, 1, 2)
        round_y(on_vector, 1, 2, 1, 0)
        round_y(on_vector, 1, 2, 1, 1)
        turn_y(1, 2, 0)
        turn_y(1, 2, 1)
        drain_y(on_scalar, 1, 2, 0)
        drain_y(on_scalar, 1, 2, 1)
        quantize_y(1, 0, 0, 2)
        store_y_words(1, 0, 0, 2)
        quantize_y(1, 1, 0, 2)
        store_y_words(1, 1, 0, 2)
        quantize_y(1, 2, 0, 1)
        store_y_words(1, 2, 0, 1)
        quantize_y(1, 2, 1, 2)
        store_y_words(1, 2, 1, 2)
        store_y_scales(1)
